import numpy as np
import ml_dtypes


def mxq(x, axis, fmt="e4m3"):
    dtype, down = {"e4m3": (ml_dtypes.float8_e4m3fn, 7), "e5m2": (ml_dtypes.float8_e5m2, 14)}[fmt]
    v = np.moveaxis(np.asarray(x, np.float32).astype(ml_dtypes.bfloat16).astype(np.float64), axis, -1)
    blocks = v.reshape(v.shape[:-1] + (-1, 32))
    amax = np.abs(blocks).max(-1, keepdims=True)
    byte = np.maximum(np.where(amax > 0, np.frexp(amax)[1] - 1 + 127, 0) - down, 1)
    scale = np.exp2(byte - 127.0)
    codes = (blocks / scale).astype(np.float32).astype(dtype).astype(np.float64)
    return np.moveaxis((codes * scale).reshape(v.shape), -1, axis)


WIDE = False


def mx_kscale(k):
    if not WIDE:
        return np.ones(k)
    levels = np.array([10, -10, 5, -5, 0])
    if k % 512:
        return np.exp2(np.random.permutation(np.resize(levels, k // 32))).repeat(32)
    a = np.empty((k // 512, 16))
    for p in range(k // 512):
        a[p, :8] = np.random.permutation(np.resize(levels, 8))
        for g in range(8):
            far = levels[np.abs(levels - a[p, g]) >= 10]
            a[p, g + 8] = far[np.random.randint(len(far))]
    return np.exp2(a.ravel()).repeat(32)


def f64(x):
    return np.asarray(x).astype(np.float64)


def striped(idx):
    return np.tile(np.asarray(idx).reshape(-1, 16).T, (8, 1)).astype(np.uint16)


def unstriped(offs):
    return offs[:16].T.reshape(-1).astype(np.int64)


E2M1 = np.array([0.0, 0.5, 1.0, 1.5, 2.0, 3.0, 4.0, 6.0, -0.0, -0.5, -1.0, -1.5, -2.0, -3.0, -4.0, -6.0])


def pack_weight(w, fmt):
    k, n = w.shape
    w = f64(np.asarray(w, np.float32).astype(ml_dtypes.bfloat16)).reshape(k // 32, 32, n)
    amax = np.abs(w).max(1)
    if fmt == "e4m3":
        byte = np.frexp(amax)[1] - 1 + 127 - 7
    else:
        mant, ex = np.frexp(amax / 6.0)
        byte = np.where(mant > 0.5, ex, ex - 1) + 127
    byte = np.clip(np.where(amax > 0, byte, 1), 1, 254)
    scaled = (w * np.exp2(127.0 - byte)[:, None, :]).reshape(k, n).astype(np.float32)
    by_word = np.ascontiguousarray(scaled.reshape(k // 512, 128, 4, n).transpose(0, 1, 3, 2))
    if fmt == "e4m3":
        words = by_word.astype(ml_dtypes.float8_e4m3fn).view(np.uint8)
    else:
        c = by_word.astype(ml_dtypes.float4_e2m1fn).view(np.uint8) & 0xF
        words = (c[..., 0::2] | (c[..., 1::2] << 4)).reshape(k // 512, 128, 2 * n)
    return np.ascontiguousarray(words), np.ascontiguousarray(byte.astype(np.uint8).reshape(k // 512, 16, n))


def unpack_weight(words, scales, fmt):
    g, _, n = scales.shape
    words = np.ascontiguousarray(words).reshape(g, 128, n, -1)
    if fmt == "e4m3":
        vals = words.view(ml_dtypes.float8_e4m3fn).astype(np.float64)
    else:
        nib = np.empty((g, 128, n, 4), np.uint8)
        nib[..., 0::2] = words & 0xF
        nib[..., 1::2] = words >> 4
        vals = E2M1[nib]
    vals = vals * np.repeat(np.exp2(scales.astype(np.float64) - 127.0), 8, axis=1)[..., None]
    return vals.transpose(0, 1, 3, 2).reshape(g * 512, n)


def e4m3fn_bytes(y):
    return np.clip(np.asarray(y, np.float64), -448.0, 448.0).astype(np.float32).astype(ml_dtypes.float8_e4m3fn).view(np.uint8)


def e4m3fn_values(b):
    return np.asarray(b, np.uint8).view(ml_dtypes.float8_e4m3fn).astype(np.float64)


K, T, J, R, F, Z, V, O, N = 512, 1024, 256, 512, 512, 1024, 1024, 128, 256


def setup_inputs():
    n = np.random.standard_normal
    idx = np.random.permutation(T)[:J]
    idx2 = np.random.permutation(Z)[:J]
    idx3 = np.random.permutation(J)[:O]
    idx4 = np.random.permutation(V)[:O]
    idx5 = np.random.permutation(J)[:O]
    fk = mx_kscale(K)
    ff = mx_kscale(F)
    fr = mx_kscale(R)
    xtp = pack_weight(n((K, T)) / fk[:, None], "e2m1")
    xop = pack_weight(n((F, Z)) / ff[:, None], "e4m3")
    wp = pack_weight(n((K, R)) * 1 / np.sqrt(K) * fk[:, None], "e4m3")
    w2p = pack_weight(n((F, R)) * 1 / np.sqrt(F) * ff[:, None] * fr, "e2m1")
    wbp = pack_weight(n((R, N)) * 1 / np.sqrt(R) / fr[:, None], "e2m1")
    return {
        "xt_words": xtp[0],
        "xt_scales": xtp[1],
        "xo_words": xop[0],
        "xo_scales": xop[1],
        "w_words": wp[0],
        "w_scales": wp[1],
        "w2_words": w2p[0],
        "w2_scales": w2p[1],
        "ca": e4m3fn_bytes(60.0 * n((R, V))),
        "st": (np.random.uniform(0.008, 0.024, (R, 1)) * fr[:, None]).astype(np.float32),
        "wb_words": wbp[0],
        "wb_scales": wbp[1],
        "offs": striped(idx),
        "offs2": striped(idx2),
        "offs3": striped(idx3),
        "offs4": striped(idx4),
        "offs5": striped(idx5),
    }


def reference(xt_words, xt_scales, xo_words, xo_scales, w_words, w_scales, w2_words, w2_scales, ca, st, wb_words, wb_scales, offs, offs2, offs3, offs4, offs5):
    idx = unstriped(offs)
    idx2 = unstriped(offs2)
    idx3 = unstriped(offs3)
    idx4 = unstriped(offs4)
    idx5 = unstriped(offs5)
    xtu = unpack_weight(xt_words, xt_scales, "e2m1")
    xou = unpack_weight(xo_words, xo_scales, "e4m3")
    wu = unpack_weight(w_words, w_scales, "e4m3")
    w2u = unpack_weight(w2_words, w2_scales, "e2m1")
    wbu = unpack_weight(wb_words, wb_scales, "e2m1")
    xtidxg = xtu[:, idx]
    a = wu.T @ xtidxg
    xoidx2g = xou[:, idx2]
    b = w2u.T @ xoidx2g
    g1 = e4m3fn_values(ca)[:, idx4] * f64(st)
    hid = np.abs(a[:, idx3] * g1 - b[:, idx5])
    hidq = mxq(hid, 0, "e4m3")
    p = wbu.T @ hidq
    return p

@@ -1,0 +1,159 @@
+from contextlib import ExitStack
+
+import concourse.mybir as mybir
+
+F32 = mybir.dt.float32
+BF16 = mybir.dt.bfloat16
+I32 = mybir.dt.int32
+U32 = mybir.dt.uint32
+U16 = mybir.dt.uint16
+U8 = mybir.dt.uint8
+FP8 = mybir.dt.float8_e4m3fn
+FP8X4 = mybir.dt.float8_e4m3fn_x4
+FP4X4 = mybir.dt.float4_e2m1fn_x4
+ALU = mybir.AluOpType
+ACT = mybir.ActivationFunctionType
+
+K, T, J, R, F, Z, V, O, N = 512, 1024, 256, 512, 512, 1024, 1024, 128, 256
+P = 128
+PACK = 4
+FLOPS = 2 * K * R * J + 2 * F * R * J + 2 * R * N * O
+
+
+def tile_list_reconciled_kernel(tc, xt_words, xt_scales, xo_words, xo_scales, w_words, w_scales, w2_words, w2_scales, ca, st, wb_words, wb_scales, offs, offs2, offs3, offs4, offs5, out):
+    nc = tc.nc
+    with ExitStack() as ctx:
+        sb = ctx.enter_context(tc.tile_pool(name="sb", bufs=1))
+        ps = ctx.enter_context(tc.psum_pool(name="ps", bufs=1))
+
+        def tile(name, shape, dtype):
+            return sb.tile(shape, dtype, name=name, align_bytes=64)
+
+        l_tok = tile("l_tok", [P, J // 16], U16)
+        l_note = tile("l_note", [P, J // 16], U16)
+        l_a = tile("l_a", [P, O // 16], U16)
+        l_gain = tile("l_gain", [P, O // 16], U16)
+        l_b = tile("l_b", [P, O // 16], U16)
+
+        xt_w = tile("xt_w", [P, T], U16)
+        xt_s = tile("xt_s", [P, T], U8)
+        xo_w = tile("xo_w", [P, Z], U32)
+        xo_s = tile("xo_s", [P, Z], U8)
+        w_w = tile("w_w", [P, R], U32)
+        w_s = tile("w_s", [P, 4 * R], U8)
+        w2_w = tile("w2_w", [P, R], U16)
+        w2_s = tile("w2_s", [P, 4 * R], U8)
+        wb_w = tile("wb_w", [P, N], U16)
+        wb_s = tile("wb_s", [P, N], U8)
+        gains = [tile("gains%d" % t, [P, V], U8) for t in range(PACK)]
+        steps = tile("steps", [P, PACK], F32)
+
+        nc.vector.memset(xt_s[:].bitcast(I32), 0)
+        nc.vector.memset(w_s[:, 0:R].bitcast(I32), 0)
+        nc.vector.memset(xo_s[:].bitcast(I32), 0)
+        nc.vector.memset(w2_s[:, 0:R].bitcast(I32), 0)
+        nc.vector.memset(wb_s[:].bitcast(I32), 0)
+
+        def load_plane(plane, scales):
+            for q in range(4):
+                nc.sync.dma_start(plane[32 * q : 32 * q + 4, :].bitcast(I32), scales[0, 4 * q : 4 * q + 4, :].bitcast(I32))
+
+        def load_rows(stage, scales):
+            nc.sync.dma_start(
+                stage[0:4, :].bitcast(I32).rearrange("r (q n) -> r q n", q=4),
+                scales[0].bitcast(I32).rearrange("(q r) n -> r q n", q=4),
+            )
+
+        nc.sync.dma_start(xt_w[:].bitcast(I32), xt_words[0].bitcast(I32))
+        nc.sync.dma_start(l_tok[:], offs)
+        load_plane(xt_s, xt_scales)
+        load_rows(w_s, w_scales)
+        nc.sync.dma_start(w_w[:].bitcast(I32), w_words[0].rearrange("p c r -> p (c r)").bitcast(I32))
+        nc.sync.dma_start(w2_w[:].bitcast(I32), w2_words[0].bitcast(I32))
+        nc.sync.dma_start(l_note[:], offs2)
+        load_plane(xo_s, xo_scales)
+        load_rows(w2_s, w2_scales)
+        nc.sync.dma_start(xo_w[:].bitcast(I32), xo_words[0].rearrange("p c r -> p (c r)").bitcast(I32))
+        nc.sync.dma_start(l_a[:], offs3)
+        nc.sync.dma_start(steps[:], st.rearrange("(p t) o -> p (t o)", t=PACK))
+        nc.sync.dma_start(l_gain[:], offs4)
+        ca_rows = ca.rearrange("(p t) v -> t p v", t=PACK)
+        for t in range(PACK):
+            nc.sync.dma_start(gains[t][:], ca_rows[t])
+        nc.sync.dma_start(l_b[:], offs5)
+        nc.sync.dma_start(wb_w[:].bitcast(I32), wb_words[0].bitcast(I32))
+        load_plane(wb_s, wb_scales)
+
+        def deal_scales(stage, dealt):
+            words = stage[:].bitcast(I32)
+            for q in range(1, 4):
+                nc.vector.tensor_copy(words[32 * q : 32 * q + 4, 0:128], words[0:4, 128 * q : 128 * (q + 1)])
+            nc.vector.tensor_copy(dealt[:].rearrange("p (t m) -> p t m", t=PACK), stage[:, 0:R].rearrange("p (m t) -> p t m", t=PACK))
+
+        xt_wg = tile("xt_wg", [P, J], U16)
+        xt_sg = tile("xt_sg", [P, J], U8)
+        nc.vector.tensor_copy(xt_wg[:], xt_w[:].indirect(l_tok[:]))
+        nc.vector.tensor_copy(xt_sg[:], xt_s[:].indirect(l_tok[:]))
+        w_sp = tile("w_sp", [P, R], U8)
+        deal_scales(w_s, w_sp)
+        w_wp = tile("w_wp", [P, R], U32)
+        nc.scalar.copy(w_wp[:].rearrange("p (t m) -> p m t", t=PACK), w_w[:].rearrange("p (m t) -> p m t", t=PACK))
+
+        a_ps = [ps.tile([P, J], F32, name="a_ps%d" % t, tag="bank%d" % t) for t in range(PACK)]
+        for t in range(PACK):
+            cols = slice(P * t, P * (t + 1))
+            nc.tensor.matmul_mx(out=a_ps[t][:], lhsT=w_wp[:, cols].bitcast(FP8X4), lhsT_scale=w_sp[:, cols], rhs=xt_wg[:].bitcast(FP4X4), rhs_scale=xt_sg[:], start=True, stop=True)
+
+        xo_wg = tile("xo_wg", [P, J], U32)
+        xo_sg = tile("xo_sg", [P, J], U8)
+        nc.vector.tensor_copy(xo_sg[:], xo_s[:].indirect(l_note[:]))
+        w2_sp = tile("w2_sp", [P, R], U8)
+        deal_scales(w2_s, w2_sp)
+        nc.vector.tensor_copy(xo_wg[:], xo_w[:].indirect(l_note[:]))
+        w2_wp = tile("w2_wp", [P, R], U16)
+        nc.scalar.copy(w2_wp[:].rearrange("p (t m) -> p t m", t=PACK), w2_w[:].rearrange("p (m t) -> p t m", t=PACK))
+
+        b_ps = [ps.tile([P, J], F32, name="b_ps%d" % t, tag="bank%d" % (PACK + t)) for t in range(PACK)]
+        for t in range(PACK):
+            cols = slice(P * t, P * (t + 1))
+            nc.tensor.matmul_mx(out=b_ps[t][:], lhsT=w2_wp[:, cols].bitcast(FP4X4), lhsT_scale=w2_sp[:, cols], rhs=xo_wg[:].bitcast(FP8X4), rhs_scale=xo_sg[:], start=True, stop=True)
+
+        a_pick = tile("a_pick", [P, PACK * O], F32)
+        g_pick = tile("g_pick", [P, PACK * O], U8)
+        prod = tile("prod", [P, PACK * O], F32)
+        diff = tile("diff", [P, PACK * O], F32)
+        a_sb = [sb.tile([P, J], F32, name="a_sb%d" % t, tag="whole%d" % t) for t in range(PACK)]
+        for t in range(PACK):
+            nc.scalar.copy(a_sb[t][:], a_ps[t][:])
+        for t in range(PACK):
+            nc.scalar.activation(a_pick[:, O * t : O * (t + 1)], a_sb[t][:].indirect(l_a[:]), ACT.Copy, scale=steps[:, t : t + 1])
+        b_sb = [sb.tile([P, J], F32, name="b_sb%d" % t, tag="whole%d" % t) for t in range(PACK)]
+        for t in range(PACK):
+            nc.scalar.copy(b_sb[t][:], b_ps[t][:])
+        for t in range(PACK):
+            nc.vector.tensor_copy(g_pick[:, O * t : O * (t + 1)], gains[t][:].indirect(l_gain[:]))
+        nc.vector.tensor_tensor(prod[:], g_pick[:].bitcast(FP8), a_pick[:], ALU.mult)
+        for t in range(PACK):
+            cols = slice(O * t, O * (t + 1))
+            nc.vector.tensor_tensor(diff[:, cols], b_sb[t][:].indirect(l_b[:]), prod[:, cols], ALU.subtract)
+
+        hid = tile("hid", [P, PACK * O], BF16)
+        hid_v = hid[:].rearrange("p (o t) -> p o t", t=PACK)
+        diff_v = diff[:].rearrange("p (t o) -> p o t", t=PACK)
+        for u in range(2):
+            nc.scalar.activation(hid_v[:, :, 2 * u : 2 * u + 2], diff_v[:, :, 2 * u : 2 * u + 2], ACT.Abs)
+        hid_w = tile("hid_w", [P, O], U32)
+        hid_s = tile("hid_s", [P, O], U8)
+        nc.vector.quantize_mx(out=hid_w[:].bitcast(FP8X4), scales=hid_s[:], in_=hid[:])
+
+        for h in range(2):
+            cols = slice(P * h, P * (h + 1))
+            o_ps = ps.tile([P, O], F32, name="o_ps%d" % h, tag="bank%d" % h)
+            nc.tensor.matmul_mx(out=o_ps[:], lhsT=wb_w[:, cols].bitcast(FP4X4), lhsT_scale=wb_s[:, cols], rhs=hid_w[:].bitcast(FP8X4), rhs_scale=hid_s[:], start=True, stop=True)
+            res = tile("res%d" % h, [P, O], F32)
+            if h == 0:
+                nc.scalar.copy(res[:], o_ps[:])
+                nc.scalar.dma_start(out[cols, :], res[:])
+            else:
+                nc.vector.tensor_copy(res[:], o_ps[:])
+                nc.sync.dma_start(out[cols, :], res[:])

@@ -40,7 +40,8 @@ def tile_list_reconciled_kernel(tc, xt_words, xt_scales, xo_words, xo_scales, w_
         xo_w = tile("xo_w", [P, Z], U32)
         xo_s = tile("xo_s", [P, Z], U8)
         w_w = tile("w_w", [P, R], U32)
-        w_s = tile("w_s", [P, 4 * R], U8)
+        w_rows = tile("w_rows", [4, 4 * R], U8)
+        w_s = tile("w_s", [P, R], U8)
         w2_w = tile("w2_w", [P, R], U16)
         w2_s = tile("w2_s", [P, 4 * R], U8)
         wb_w = tile("wb_w", [P, N], U16)
@@ -49,14 +50,14 @@ def tile_list_reconciled_kernel(tc, xt_words, xt_scales, xo_words, xo_scales, w_
         steps = tile("steps", [P, PACK], F32)
 
         nc.vector.memset(xt_s[:].bitcast(I32), 0)
-        nc.vector.memset(w_s[:, 0:R].bitcast(I32), 0)
+        nc.vector.memset(w_s[:].bitcast(I32), 0)
         nc.vector.memset(xo_s[:].bitcast(I32), 0)
         nc.vector.memset(w2_s[:, 0:R].bitcast(I32), 0)
         nc.vector.memset(wb_s[:].bitcast(I32), 0)
 
         def load_plane(plane, scales):
-            for q in range(4):
-                nc.sync.dma_start(plane[32 * q : 32 * q + 4, :].bitcast(I32), scales[0, 4 * q : 4 * q + 4, :].bitcast(I32))
+            for r in range(4):
+                nc.sync.dma_start(plane[r:P:32, :].bitcast(I32), scales[0, r:16:4, :].bitcast(I32))
 
         def load_rows(stage, scales):
             nc.sync.dma_start(
@@ -64,38 +65,40 @@ def tile_list_reconciled_kernel(tc, xt_words, xt_scales, xo_words, xo_scales, w_
                 scales[0].bitcast(I32).rearrange("(q r) n -> r q n", q=4),
             )
 
-        nc.sync.dma_start(xt_w[:].bitcast(I32), xt_words[0].bitcast(I32))
+        ca_rows = ca.rearrange("(p t) v -> t p v", t=PACK)
+        load_rows(w_rows, w_scales)
         nc.sync.dma_start(l_tok[:], offs)
+        nc.sync.dma_start(xt_w[:].bitcast(I32), xt_words[0].bitcast(I32))
         load_plane(xt_s, xt_scales)
-        load_rows(w_s, w_scales)
         nc.sync.dma_start(w_w[:].bitcast(I32), w_words[0].rearrange("p c r -> p (c r)").bitcast(I32))
         nc.sync.dma_start(w2_w[:].bitcast(I32), w2_words[0].bitcast(I32))
+        load_rows(w2_s, w2_scales)
         nc.sync.dma_start(l_note[:], offs2)
         load_plane(xo_s, xo_scales)
-        load_rows(w2_s, w2_scales)
         nc.sync.dma_start(xo_w[:].bitcast(I32), xo_words[0].rearrange("p c r -> p (c r)").bitcast(I32))
         nc.sync.dma_start(l_a[:], offs3)
         nc.sync.dma_start(steps[:], st.rearrange("(p t) o -> p (t o)", t=PACK))
         nc.sync.dma_start(l_gain[:], offs4)
-        ca_rows = ca.rearrange("(p t) v -> t p v", t=PACK)
         for t in range(PACK):
             nc.sync.dma_start(gains[t][:], ca_rows[t])
         nc.sync.dma_start(l_b[:], offs5)
         nc.sync.dma_start(wb_w[:].bitcast(I32), wb_words[0].bitcast(I32))
         load_plane(wb_s, wb_scales)
 
-        def deal_scales(stage, dealt):
-            words = stage[:].bitcast(I32)
-            for q in range(1, 4):
-                nc.vector.tensor_copy(words[32 * q : 32 * q + 4, 0:128], words[0:4, 128 * q : 128 * (q + 1)])
-            nc.vector.tensor_copy(dealt[:].rearrange("p (t m) -> p t m", t=PACK), stage[:, 0:R].rearrange("p (m t) -> p t m", t=PACK))
+        def spread_rows(rows, plane, first):
+            for q in range(first, 4):
+                nc.vector.tensor_copy(plane[:].bitcast(I32)[32 * q : 32 * q + 4, 0:128], rows[:].bitcast(I32)[0:4, 128 * q : 128 * (q + 1)])
+
+        def deal_scales(plane, dealt):
+            nc.vector.tensor_copy(dealt[:].rearrange("p (t m) -> p t m", t=PACK), plane[:, 0:R].rearrange("p (m t) -> p t m", t=PACK))
 
         xt_wg = tile("xt_wg", [P, J], U16)
         xt_sg = tile("xt_sg", [P, J], U8)
-        nc.vector.tensor_copy(xt_wg[:], xt_w[:].indirect(l_tok[:]))
-        nc.vector.tensor_copy(xt_sg[:], xt_s[:].indirect(l_tok[:]))
         w_sp = tile("w_sp", [P, R], U8)
+        spread_rows(w_rows, w_s, 0)
+        nc.vector.tensor_copy(xt_wg[:], xt_w[:].indirect(l_tok[:]))
         deal_scales(w_s, w_sp)
+        nc.vector.tensor_copy(xt_sg[:], xt_s[:].indirect(l_tok[:]))
         w_wp = tile("w_wp", [P, R], U32)
         nc.scalar.copy(w_wp[:].rearrange("p (t m) -> p m t", t=PACK), w_w[:].rearrange("p (m t) -> p m t", t=PACK))
 
@@ -106,8 +109,9 @@ def tile_list_reconciled_kernel(tc, xt_words, xt_scales, xo_words, xo_scales, w_
 
         xo_wg = tile("xo_wg", [P, J], U32)
         xo_sg = tile("xo_sg", [P, J], U8)
-        nc.vector.tensor_copy(xo_sg[:], xo_s[:].indirect(l_note[:]))
         w2_sp = tile("w2_sp", [P, R], U8)
+        spread_rows(w2_s, w2_s, 1)
+        nc.vector.tensor_copy(xo_sg[:], xo_s[:].indirect(l_note[:]))
         deal_scales(w2_s, w2_sp)
         nc.vector.tensor_copy(xo_wg[:], xo_w[:].indirect(l_note[:]))
         w2_wp = tile("w2_wp", [P, R], U16)
@@ -132,7 +136,9 @@ def tile_list_reconciled_kernel(tc, xt_words, xt_scales, xo_words, xo_scales, w_
             nc.scalar.copy(b_sb[t][:], b_ps[t][:])
         for t in range(PACK):
             nc.vector.tensor_copy(g_pick[:, O * t : O * (t + 1)], gains[t][:].indirect(l_gain[:]))
-        nc.vector.tensor_tensor(prod[:], g_pick[:].bitcast(FP8), a_pick[:], ALU.mult)
+        for u in range(2):
+            cols = slice(2 * O * u, 2 * O * (u + 1))
+            nc.vector.tensor_tensor(prod[:, cols], g_pick[:, cols].bitcast(FP8), a_pick[:, cols], ALU.mult)
         for t in range(PACK):
             cols = slice(O * t, O * (t + 1))
             nc.vector.tensor_tensor(diff[:, cols], b_sb[t][:].indirect(l_b[:]), prod[:, cols], ALU.subtract)

@@ -139,15 +139,24 @@ def tile_list_reconciled_kernel(tc, xt_words, xt_scales, xo_words, xo_scales, w_
         for u in range(2):
             cols = slice(2 * O * u, 2 * O * (u + 1))
             nc.vector.tensor_tensor(prod[:, cols], g_pick[:, cols].bitcast(FP8), a_pick[:, cols], ALU.mult)
-        for t in range(PACK):
+        b_pick = tile("b_pick", [P, 2 * O], F32)
+        for t in range(2):
             cols = slice(O * t, O * (t + 1))
             nc.vector.tensor_tensor(diff[:, cols], b_sb[t][:].indirect(l_b[:]), prod[:, cols], ALU.subtract)
+            nc.scalar.activation(b_pick[:, cols], b_sb[2 + t][:].indirect(l_b[:]), ACT.Copy)
+        diff_t = diff[:].rearrange("p (t o) -> p t o", t=PACK)
+        prod_t = prod[:].rearrange("p (t o) -> p t o", t=PACK)
+        b_pick_t = b_pick[:].rearrange("p (t o) -> p t o", t=2)
+        for u in range(2):
+            half = slice(64 * u, 64 * (u + 1))
+            nc.vector.tensor_tensor(diff_t[:, 2:4, half], b_pick_t[:, :, half], prod_t[:, 2:4, half], ALU.subtract)
 
         hid = tile("hid", [P, PACK * O], BF16)
         hid_v = hid[:].rearrange("p (o t) -> p o t", t=PACK)
         diff_v = diff[:].rearrange("p (t o) -> p o t", t=PACK)
         for u in range(2):
-            nc.scalar.activation(hid_v[:, :, 2 * u : 2 * u + 2], diff_v[:, :, 2 * u : 2 * u + 2], ACT.Abs)
+            half = slice(64 * u, 64 * (u + 1))
+            nc.scalar.activation(hid_v[:, half, :], diff_v[:, half, :], ACT.Abs)
         hid_w = tile("hid_w", [P, O], U32)
         hid_s = tile("hid_s", [P, O], U8)
         nc.vector.quantize_mx(out=hid_w[:].bitcast(FP8X4), scales=hid_s[:], in_=hid[:])

from contextlib import ExitStack

import concourse.mybir as mybir

F32 = mybir.dt.float32
BF16 = mybir.dt.bfloat16
I32 = mybir.dt.int32
U32 = mybir.dt.uint32
U16 = mybir.dt.uint16
U8 = mybir.dt.uint8
FP8 = mybir.dt.float8_e4m3fn
FP8X4 = mybir.dt.float8_e4m3fn_x4
FP4X4 = mybir.dt.float4_e2m1fn_x4
ALU = mybir.AluOpType
ACT = mybir.ActivationFunctionType

K, T, J, R, F, Z, V, O, N = 512, 1024, 256, 512, 512, 1024, 1024, 128, 256
P = 128
PACK = 4
FLOPS = 2 * K * R * J + 2 * F * R * J + 2 * R * N * O


def tile_list_reconciled_kernel(tc, xt_words, xt_scales, xo_words, xo_scales, w_words, w_scales, w2_words, w2_scales, ca, st, wb_words, wb_scales, offs, offs2, offs3, offs4, offs5, out):
    nc = tc.nc
    with ExitStack() as ctx:
        sb = ctx.enter_context(tc.tile_pool(name="sb", bufs=1))
        ps = ctx.enter_context(tc.psum_pool(name="ps", bufs=1))

        def tile(name, shape, dtype):
            return sb.tile(shape, dtype, name=name, align_bytes=64)

        l_tok = tile("l_tok", [P, J // 16], U16)
        l_note = tile("l_note", [P, J // 16], U16)
        l_a = tile("l_a", [P, O // 16], U16)
        l_gain = tile("l_gain", [P, O // 16], U16)
        l_b = tile("l_b", [P, O // 16], U16)

        xt_w = tile("xt_w", [P, T], U16)
        xt_s = tile("xt_s", [P, T], U8)
        xo_w = tile("xo_w", [P, Z], U32)
        xo_s = tile("xo_s", [P, Z], U8)
        w_w = tile("w_w", [P, R], U32)
        w_rows = tile("w_rows", [4, 4 * R], U8)
        w_s = tile("w_s", [P, R], U8)
        w2_w = tile("w2_w", [P, R], U16)
        w2_s = tile("w2_s", [P, 4 * R], U8)
        wb_w = tile("wb_w", [P, N], U16)
        wb_s = tile("wb_s", [P, N], U8)
        gains = [tile("gains%d" % t, [P, V], U8) for t in range(PACK)]
        steps = tile("steps", [P, PACK], F32)

        nc.vector.memset(xt_s[:].bitcast(I32), 0)
        nc.vector.memset(w_s[:].bitcast(I32), 0)
        nc.vector.memset(xo_s[:].bitcast(I32), 0)
        nc.vector.memset(w2_s[:, 0:R].bitcast(I32), 0)
        nc.vector.memset(wb_s[:].bitcast(I32), 0)

        def load_plane(plane, scales):
            for r in range(4):
                nc.sync.dma_start(plane[r:P:32, :].bitcast(I32), scales[0, r:16:4, :].bitcast(I32))

        def load_rows(stage, scales):
            nc.sync.dma_start(
                stage[0:4, :].bitcast(I32).rearrange("r (q n) -> r q n", q=4),
                scales[0].bitcast(I32).rearrange("(q r) n -> r q n", q=4),
            )

        ca_rows = ca.rearrange("(p t) v -> t p v", t=PACK)
        load_rows(w_rows, w_scales)
        nc.sync.dma_start(l_tok[:], offs)
        nc.sync.dma_start(xt_w[:].bitcast(I32), xt_words[0].bitcast(I32))
        load_plane(xt_s, xt_scales)
        nc.sync.dma_start(w_w[:].bitcast(I32), w_words[0].rearrange("p c r -> p (c r)").bitcast(I32))
        nc.sync.dma_start(w2_w[:].bitcast(I32), w2_words[0].bitcast(I32))
        load_rows(w2_s, w2_scales)
        nc.sync.dma_start(l_note[:], offs2)
        load_plane(xo_s, xo_scales)
        nc.sync.dma_start(xo_w[:].bitcast(I32), xo_words[0].rearrange("p c r -> p (c r)").bitcast(I32))
        nc.sync.dma_start(l_a[:], offs3)
        nc.sync.dma_start(steps[:], st.rearrange("(p t) o -> p (t o)", t=PACK))
        nc.sync.dma_start(l_gain[:], offs4)
        for t in range(PACK):
            nc.sync.dma_start(gains[t][:], ca_rows[t])
        nc.sync.dma_start(l_b[:], offs5)
        nc.sync.dma_start(wb_w[:].bitcast(I32), wb_words[0].bitcast(I32))
        load_plane(wb_s, wb_scales)

        def spread_rows(rows, plane, first):
            for q in range(first, 4):
                nc.vector.tensor_copy(plane[:].bitcast(I32)[32 * q : 32 * q + 4, 0:128], rows[:].bitcast(I32)[0:4, 128 * q : 128 * (q + 1)])

        def deal_scales(plane, dealt):
            nc.vector.tensor_copy(dealt[:].rearrange("p (t m) -> p t m", t=PACK), plane[:, 0:R].rearrange("p (m t) -> p t m", t=PACK))

        xt_wg = tile("xt_wg", [P, J], U16)
        xt_sg = tile("xt_sg", [P, J], U8)
        w_sp = tile("w_sp", [P, R], U8)
        spread_rows(w_rows, w_s, 0)
        nc.vector.tensor_copy(xt_wg[:], xt_w[:].indirect(l_tok[:]))
        deal_scales(w_s, w_sp)
        nc.vector.tensor_copy(xt_sg[:], xt_s[:].indirect(l_tok[:]))
        w_wp = tile("w_wp", [P, R], U32)
        nc.scalar.copy(w_wp[:].rearrange("p (t m) -> p m t", t=PACK), w_w[:].rearrange("p (m t) -> p m t", t=PACK))

        a_ps = [ps.tile([P, J], F32, name="a_ps%d" % t, tag="bank%d" % t) for t in range(PACK)]
        for t in range(PACK):
            cols = slice(P * t, P * (t + 1))
            nc.tensor.matmul_mx(out=a_ps[t][:], lhsT=w_wp[:, cols].bitcast(FP8X4), lhsT_scale=w_sp[:, cols], rhs=xt_wg[:].bitcast(FP4X4), rhs_scale=xt_sg[:], start=True, stop=True)

        xo_wg = tile("xo_wg", [P, J], U32)
        xo_sg = tile("xo_sg", [P, J], U8)
        w2_sp = tile("w2_sp", [P, R], U8)
        spread_rows(w2_s, w2_s, 1)
        nc.vector.tensor_copy(xo_sg[:], xo_s[:].indirect(l_note[:]))
        deal_scales(w2_s, w2_sp)
        nc.vector.tensor_copy(xo_wg[:], xo_w[:].indirect(l_note[:]))
        w2_wp = tile("w2_wp", [P, R], U16)
        nc.scalar.copy(w2_wp[:].rearrange("p (t m) -> p t m", t=PACK), w2_w[:].rearrange("p (m t) -> p t m", t=PACK))

        b_ps = [ps.tile([P, J], F32, name="b_ps%d" % t, tag="bank%d" % (PACK + t)) for t in range(PACK)]
        for t in range(PACK):
            cols = slice(P * t, P * (t + 1))
            nc.tensor.matmul_mx(out=b_ps[t][:], lhsT=w2_wp[:, cols].bitcast(FP4X4), lhsT_scale=w2_sp[:, cols], rhs=xo_wg[:].bitcast(FP8X4), rhs_scale=xo_sg[:], start=True, stop=True)

        a_pick = tile("a_pick", [P, PACK * O], F32)
        g_pick = tile("g_pick", [P, PACK * O], U8)
        prod = tile("prod", [P, PACK * O], F32)
        diff = tile("diff", [P, PACK * O], F32)
        a_sb = [sb.tile([P, J], F32, name="a_sb%d" % t, tag="whole%d" % t) for t in range(PACK)]
        for t in range(PACK):
            nc.scalar.copy(a_sb[t][:], a_ps[t][:])
        for t in range(PACK):
            nc.scalar.activation(a_pick[:, O * t : O * (t + 1)], a_sb[t][:].indirect(l_a[:]), ACT.Copy, scale=steps[:, t : t + 1])
        b_sb = [sb.tile([P, J], F32, name="b_sb%d" % t, tag="whole%d" % t) for t in range(PACK)]
        for t in range(PACK):
            nc.scalar.copy(b_sb[t][:], b_ps[t][:])
        for t in range(PACK):
            nc.vector.tensor_copy(g_pick[:, O * t : O * (t + 1)], gains[t][:].indirect(l_gain[:]))
        for u in range(2):
            cols = slice(2 * O * u, 2 * O * (u + 1))
            nc.vector.tensor_tensor(prod[:, cols], g_pick[:, cols].bitcast(FP8), a_pick[:, cols], ALU.mult)
        b_pick = tile("b_pick", [P, 2 * O], F32)
        for t in range(2):
            cols = slice(O * t, O * (t + 1))
            nc.vector.tensor_tensor(diff[:, cols], b_sb[t][:].indirect(l_b[:]), prod[:, cols], ALU.subtract)
            nc.scalar.activation(b_pick[:, cols], b_sb[2 + t][:].indirect(l_b[:]), ACT.Copy)
        diff_t = diff[:].rearrange("p (t o) -> p t o", t=PACK)
        prod_t = prod[:].rearrange("p (t o) -> p t o", t=PACK)
        b_pick_t = b_pick[:].rearrange("p (t o) -> p t o", t=2)
        for u in range(2):
            half = slice(64 * u, 64 * (u + 1))
            nc.vector.tensor_tensor(diff_t[:, 2:4, half], b_pick_t[:, :, half], prod_t[:, 2:4, half], ALU.subtract)

        hid = tile("hid", [P, PACK * O], BF16)
        hid_v = hid[:].rearrange("p (o t) -> p o t", t=PACK)
        diff_v = diff[:].rearrange("p (t o) -> p o t", t=PACK)
        for u in range(2):
            half = slice(64 * u, 64 * (u + 1))
            nc.scalar.activation(hid_v[:, half, :], diff_v[:, half, :], ACT.Abs)
        hid_w = tile("hid_w", [P, O], U32)
        hid_s = tile("hid_s", [P, O], U8)
        nc.vector.quantize_mx(out=hid_w[:].bitcast(FP8X4), scales=hid_s[:], in_=hid[:])

        for h in range(2):
            cols = slice(P * h, P * (h + 1))
            o_ps = ps.tile([P, O], F32, name="o_ps%d" % h, tag="bank%d" % h)
            nc.tensor.matmul_mx(out=o_ps[:], lhsT=wb_w[:, cols].bitcast(FP4X4), lhsT_scale=wb_s[:, cols], rhs=hid_w[:].bitcast(FP8X4), rhs_scale=hid_s[:], start=True, stop=True)
            res = tile("res%d" % h, [P, O], F32)
            if h == 0:
                nc.scalar.copy(res[:], o_ps[:])
                nc.scalar.dma_start(out[cols, :], res[:])
            else:
                nc.vector.tensor_copy(res[:], o_ps[:])
                nc.sync.dma_start(out[cols, :], res[:])
